import numpy as np
import ml_dtypes


def mxq(x, axis, fmt="e4m3"):
    dtype, down = {"e4m3": (ml_dtypes.float8_e4m3fn, 7), "e5m2": (ml_dtypes.float8_e5m2, 14)}[fmt]
    v = np.moveaxis(np.asarray(x, np.float32).astype(ml_dtypes.bfloat16).astype(np.float64), axis, -1)
    blocks = v.reshape(v.shape[:-1] + (-1, 32))
    amax = np.abs(blocks).max(-1, keepdims=True)
    byte = np.maximum(np.where(amax > 0, np.frexp(amax)[1] - 1 + 127, 0) - down, 1)
    scale = np.exp2(byte - 127.0)
    codes = (blocks / scale).astype(np.float32).astype(dtype).astype(np.float64)
    return np.moveaxis((codes * scale).reshape(v.shape), -1, axis)


WIDE = False


def mx_kscale(k):
    if not WIDE:
        return np.ones(k)
    levels = np.array([30, -30])
    if k % 512:
        return np.exp2(np.random.permutation(np.resize(levels, k // 32))).repeat(32)
    a = np.empty((k // 512, 16))
    for p in range(k // 512):
        a[p, :8] = np.random.permutation(np.resize(levels, 8))
        for g in range(8):
            far = levels[np.abs(levels - a[p, g]) >= 10]
            a[p, g + 8] = far[np.random.randint(len(far))]
    return np.exp2(a.ravel()).repeat(32)


def f64(x):
    return np.asarray(x).astype(np.float64)


def striped(idx):
    return np.tile(np.asarray(idx).reshape(-1, 16).T, (8, 1)).astype(np.uint16)


def unstriped(offs):
    return offs[:16].T.reshape(-1).astype(np.int64)


E2M1 = np.array([0.0, 0.5, 1.0, 1.5, 2.0, 3.0, 4.0, 6.0, -0.0, -0.5, -1.0, -1.5, -2.0, -3.0, -4.0, -6.0])


def pack_weight(w, fmt):
    k, n = w.shape
    w = f64(np.asarray(w, np.float32).astype(ml_dtypes.bfloat16)).reshape(k // 32, 32, n)
    amax = np.abs(w).max(1)
    if fmt == "e4m3":
        byte = np.frexp(amax)[1] - 1 + 127 - 7
    else:
        mant, ex = np.frexp(amax / 6.0)
        byte = np.where(mant > 0.5, ex, ex - 1) + 127
    byte = np.clip(np.where(amax > 0, byte, 1), 1, 254)
    scaled = (w * np.exp2(127.0 - byte)[:, None, :]).reshape(k, n).astype(np.float32)
    by_word = np.ascontiguousarray(scaled.reshape(k // 512, 128, 4, n).transpose(0, 1, 3, 2))
    if fmt == "e4m3":
        words = by_word.astype(ml_dtypes.float8_e4m3fn).view(np.uint8)
    else:
        c = by_word.astype(ml_dtypes.float4_e2m1fn).view(np.uint8) & 0xF
        words = (c[..., 0::2] | (c[..., 1::2] << 4)).reshape(k // 512, 128, 2 * n)
    return np.ascontiguousarray(words), np.ascontiguousarray(byte.astype(np.uint8).reshape(k // 512, 16, n))


def unpack_weight(words, scales, fmt):
    g, _, n = scales.shape
    words = np.ascontiguousarray(words).reshape(g, 128, n, -1)
    if fmt == "e4m3":
        vals = words.view(ml_dtypes.float8_e4m3fn).astype(np.float64)
    else:
        nib = np.empty((g, 128, n, 4), np.uint8)
        nib[..., 0::2] = words & 0xF
        nib[..., 1::2] = words >> 4
        vals = E2M1[nib]
    vals = vals * np.repeat(np.exp2(scales.astype(np.float64) - 127.0), 8, axis=1)[..., None]
    return vals.transpose(0, 1, 3, 2).reshape(g * 512, n)


def sigmoid(v):
    return 1.0 / (1.0 + np.exp(-v))


def sgn(shape):
    return np.random.uniform(0.5, 2.0, shape) * np.where(np.random.standard_normal(shape) < 0, -1.0, 1.0)


K, T, J, R, F, Z, O, N, E = 512, 1024, 256, 512, 512, 1024, 128, 256, 512


def setup_inputs():
    n = np.random.standard_normal
    idx = np.random.permutation(T)[:J]
    idx2 = np.random.permutation(Z)[:J]
    idx3 = np.random.permutation(J)[:O]
    idx4 = np.random.permutation(J)[:O]
    idx5 = np.random.permutation(J)[:O]
    idx6 = np.random.permutation(E)[:O]
    idx7 = np.random.permutation(E)[:O]
    fk = mx_kscale(K)
    ff = mx_kscale(F)
    fr = mx_kscale(R)
    xtp = pack_weight(n((K, T)) / fk[:, None], "e2m1")
    xop = pack_weight(n((F, Z)) / ff[:, None], "e4m3")
    wp = pack_weight(n((K, R)) * 1 / np.sqrt(K) * fk[:, None], "e4m3")
    w0p = pack_weight(n((F, R)) * 1 / np.sqrt(F) * ff[:, None], "e2m1")
    wbp = pack_weight(n((R, N)) * 1 / np.sqrt(R) / fr[:, None], "e2m1")
    return {
        "xt_words": xtp[0],
        "xt_scales": xtp[1],
        "xo_words": xop[0],
        "xo_scales": xop[1],
        "w_words": wp[0],
        "w_scales": wp[1],
        "w0_words": w0p[0],
        "w0_scales": w0p[1],
        "sa": (np.random.uniform(0.5, 1.6, (R, 1)) * fr[:, None]).astype(np.float32),
        "sb": (np.random.uniform(0.5, 1.6, (R, 1)) * fr[:, None]).astype(np.float32),
        "sg": (sgn((R, 1))).astype(np.float32),
        "bg": (np.random.uniform(-2.0, 2.0, (R, 1))).astype(np.float32),
        "wb_words": wbp[0],
        "wb_scales": wbp[1],
        "offs": striped(idx),
        "offs2": striped(idx2),
        "offs3": striped(idx3),
        "offs4": striped(idx4),
        "offs5": striped(idx5),
        "offs6": striped(idx6),
        "offs7": striped(idx7),
    }


def reference(xt_words, xt_scales, xo_words, xo_scales, w_words, w_scales, w0_words, w0_scales, sa, sb, sg, bg, wb_words, wb_scales, offs, offs2, offs3, offs4, offs5, offs6, offs7):
    idx = unstriped(offs)
    idx2 = unstriped(offs2)
    idx3 = unstriped(offs3)
    idx4 = unstriped(offs4)
    idx5 = unstriped(offs5)
    idx6 = unstriped(offs6)
    idx7 = unstriped(offs7)
    xtu = unpack_weight(xt_words, xt_scales, "e2m1")
    xou = unpack_weight(xo_words, xo_scales, "e4m3")
    wu = unpack_weight(w_words, w_scales, "e4m3")
    w0u = unpack_weight(w0_words, w0_scales, "e2m1")
    wbu = unpack_weight(wb_words, wb_scales, "e2m1")
    xtidxg = xtu[:, idx]
    xoidx2g = xou[:, idx2]
    a = wu.T @ xtidxg + w0u.T @ xoidx2g
    hid = np.abs(a[:, idx3] * f64(sa) * sigmoid(a[:, idx4] * f64(sg) + f64(bg)) - a[:, idx5] * f64(sb))
    hidq = mxq(hid, 0, "e5m2")
    p = wbu.T @ hidq
    pa = np.zeros((N, E))
    pa[:, idx6] = p
    pb = np.zeros((N, E))
    pb[:, idx7] = p
    y = pa + pb
    return y

@@ -1,0 +1,193 @@
+from contextlib import ExitStack
+
+import concourse.mybir as mybir
+
+K, T, J, R, F, Z, O, N, E = 512, 1024, 256, 512, 512, 1024, 128, 256, 512
+FLOPS = 2 * K * R * J + 2 * F * R * J + 2 * R * N * O
+
+F32 = mybir.dt.float32
+BF16 = mybir.dt.bfloat16
+I32 = mybir.dt.int32
+U32 = mybir.dt.uint32
+U16 = mybir.dt.uint16
+U8 = mybir.dt.uint8
+E4M3 = mybir.dt.float8_e4m3fn_x4
+E5M2 = mybir.dt.float8_e5m2_x4
+E2M1 = mybir.dt.float4_e2m1fn_x4
+ACT = mybir.ActivationFunctionType
+ALU = mybir.AluOpType
+
+P = 128
+PACK = 4
+QUADS = 4
+POOL_COLS = 384
+
+
+def tile_list_gatedless_bank_one_pagetwice_kernel(
+    tc, xt_words, xt_scales, xo_words, xo_scales, w_words, w_scales, w0_words, w0_scales,
+    sa, sb, sg, bg, wb_words, wb_scales, offs, offs2, offs3, offs4, offs5, offs6, offs7, out,
+):
+    nc = tc.nc
+    with ExitStack() as ctx:
+        keep = ctx.enter_context(tc.tile_pool(name="keep", bufs=1))
+        psum = ctx.enter_context(tc.psum_pool(name="psum", bufs=1))
+
+        def sbuf(name, shape, dtype):
+            return keep.tile(shape, dtype, name=name, align_bytes=64)
+
+        def load_list(name, src):
+            tile = keep.tile(list(src.shape), U16, name=name)
+            nc.sync.dma_start(tile[:], src)
+            return tile
+
+        def load_rows(name, src, queue):
+            tile = sbuf(name, [P, PACK], F32)
+            queue.dma_start(tile[:], src.rearrange("(p t) one -> p (t one)", t=PACK))
+            return tile
+
+        def load_scale_rows(plane, src, quads, queue):
+            rows = src[0].bitcast(I32)
+            for q in quads:
+                queue.dma_start(plane[:].bitcast(I32)[32 * q : 32 * q + 4, :], rows[4 * q : 4 * q + 4, :])
+
+        xo_stage = sbuf("xo_stage", [P // 2, 2, Z // 4], I32)
+        xt_plane = sbuf("xt_plane", [P, T], U8)
+        w_raw = sbuf("w_raw", [P, 2 * R], U8)
+        wb_plane = sbuf("wb_plane", [P, N], U8)
+        nc.gpsimd.memset(xo_stage[:], 0)
+        for plane in (xt_plane, w_raw, wb_plane):
+            nc.vector.memset(plane[:].bitcast(I32), 0)
+
+        l2 = load_list("l2", offs2)
+        l1 = load_list("l1", offs)
+        xo_all = sbuf("xo_all", [P, Z], I32)
+        nc.sync.dma_start(xo_all[:], xo_words[0].rearrange("p c i -> p (c i)").bitcast(I32))
+        xt_all = sbuf("xt_all", [P, T], U16)
+        nc.sync.dma_start(xt_all[:].bitcast(I32), xt_words[0].bitcast(I32))
+        stage = sbuf("stage", [4, QUADS, 2 * R // 4], I32)
+        nc.scalar.dma_start(stage[:, :, 0 : R // 4], w0_scales[0].bitcast(I32).rearrange("(q i) c -> i q c", i=4))
+        nc.scalar.dma_start(stage[:, :, R // 4 :], w_scales[0].bitcast(I32).rearrange("(q i) c -> i q c", i=4))
+        xo_rows = xo_scales[0].bitcast(I32).rearrange("(u v i) c -> v i u c", u=2, v=2)
+        for v in range(2):
+            nc.scalar.dma_start(xo_stage[32 * v : 32 * v + 4, :, :], xo_rows[v])
+        w0_all = sbuf("w0_all", [P, R], U16)
+        nc.sync.dma_start(w0_all[:].bitcast(I32), w0_words[0].bitcast(I32))
+        w_all = sbuf("w_all", [P, R], I32)
+        nc.sync.dma_start(w_all[:], w_words[0].rearrange("p c i -> p (c i)").bitcast(I32))
+        load_scale_rows(xt_plane, xt_scales, range(QUADS), nc.sync)
+        l4 = load_list("l4", offs4)
+        sg_t = load_rows("sg_t", sg, nc.sync)
+        bg_t = load_rows("bg_t", bg, nc.sync)
+        l3 = load_list("l3", offs3)
+        sa_t = load_rows("sa_t", sa, nc.sync)
+        l5 = load_list("l5", offs5)
+        sb_t = load_rows("sb_t", sb, nc.sync)
+        wb_all = sbuf("wb_all", [P, 2 * N], U8)
+        nc.sync.dma_start(wb_all[:].bitcast(I32), wb_words[0].bitcast(I32))
+        load_scale_rows(wb_plane, wb_scales, range(QUADS), nc.sync)
+        l6 = load_list("l6", offs6)
+        l7 = load_list("l7", offs7)
+
+        pages = [[sbuf("page%d%d" % (h, s), [P, E], F32) for s in range(2)] for h in range(2)]
+        for s in range(2):
+            nc.vector.memset(pages[0][s][:], 0.0)
+            nc.gpsimd.memset(pages[1][s][:], 0.0)
+
+        for q in range(QUADS):
+            nc.vector.tensor_copy(w_raw[:].bitcast(I32)[32 * q : 32 * q + 4, :], stage[:, q, :])
+        w0_plane = sbuf("w0_plane", [P, R], U8)
+        w_plane = sbuf("w_plane", [P, R], U8)
+        for plane, c0 in ((w0_plane, 0), (w_plane, R)):
+            nc.gpsimd.tensor_copy(
+                plane[:].rearrange("p (t m) -> p t m", t=PACK),
+                w_raw[:, c0 : c0 + R].rearrange("p (m t) -> p t m", t=PACK),
+            )
+        w0_codes = sbuf("w0_codes", [P, R], U16)
+        nc.scalar.copy(
+            w0_codes[:].rearrange("p (t m) -> p m t", t=PACK), w0_all[:].rearrange("p (m t) -> p m t", t=PACK)
+        )
+        w_codes = sbuf("w_codes", [P, R], U32)
+        nc.scalar.copy(
+            w_codes[:].rearrange("p (t m) -> p m t", t=PACK),
+            w_all[:].bitcast(U32).rearrange("p (m t) -> p m t", t=PACK),
+        )
+
+        xo_plane = sbuf("xo_plane", [P, Z], U8)
+        for u in range(2):
+            nc.vector.tensor_copy(xo_plane[:].bitcast(I32)[64 * u : 64 * (u + 1), :], xo_stage[:, u, :])
+        xo_picked = sbuf("xo_picked", [P, J], U8)
+        nc.vector.tensor_copy(xo_picked[:], xo_plane[:].indirect(l2[:]))
+        xo_codes = sbuf("xo_codes", [P, J], U32)
+        nc.vector.tensor_copy(xo_codes[:], xo_all[:].bitcast(U32).indirect(l2[:]))
+        xt_codes = sbuf("xt_codes", [P, J], U16)
+        nc.vector.tensor_copy(xt_codes[:], xt_all[:].indirect(l1[:]))
+        xt_picked = sbuf("xt_picked", [P, J], U8)
+        nc.vector.tensor_copy(xt_picked[:], xt_plane[:].indirect(l1[:]))
+
+        banks = [psum.tile([P, J], F32, name="a_bank%d" % t) for t in range(PACK)]
+        for t in range(PACK):
+            cols = slice(t * P, (t + 1) * P)
+            nc.tensor.matmul_mx(
+                banks[t][:], lhsT=w0_codes[:, cols].bitcast(E2M1), lhsT_scale=w0_plane[:, cols],
+                rhs=xo_codes[:].bitcast(E4M3), rhs_scale=xo_picked[:], start=True, stop=False,
+            )
+            nc.tensor.matmul_mx(
+                banks[t][:], lhsT=w_codes[:, cols].bitcast(E4M3), lhsT_scale=w_plane[:, cols],
+                rhs=xt_codes[:].bitcast(E2M1), rhs_scale=xt_picked[:], start=False, stop=True,
+            )
+
+        gate = sbuf("gate", [P, PACK, O], F32)
+        first = sbuf("first", [P, PACK, O], F32)
+        second = sbuf("second", [P, PACK, O], F32)
+        gated = sbuf("gated", [P, PACK, O], F32)
+        diff = sbuf("diff", [P, PACK, O], F32)
+        a_rows = [sbuf("a_rows%d" % t, [P, J], F32) for t in range(PACK)]
+        for t in range(PACK):
+            nc.vector.tensor_copy(a_rows[t][:], banks[t][:])
+        for t in range(PACK):
+            col = slice(t, t + 1)
+            nc.scalar.activation(
+                gate[:, t, :], a_rows[t][:].indirect(l4[:]), ACT.Sigmoid, bias=bg_t[:, col], scale=sg_t[:, col]
+            )
+            nc.scalar.activation(first[:, t, :], a_rows[t][:].indirect(l3[:]), ACT.Copy, scale=sa_t[:, col])
+            nc.vector.tensor_tensor(gated[:, t, :], first[:, t, :], gate[:, t, :], ALU.mult)
+            nc.scalar.activation(second[:, t, :], a_rows[t][:].indirect(l5[:]), ACT.Copy, scale=sb_t[:, col])
+            nc.vector.tensor_tensor(diff[:, t, :], gated[:, t, :], second[:, t, :], ALU.subtract)
+
+        hid = sbuf("hid", [P, O, PACK], BF16)
+        woven = diff[:].rearrange("p t o -> p o t")
+        lo, hi = slice(0, O // 2), slice(O // 2, O)
+        nc.scalar.activation(hid[:, hi, :], woven[:, hi, :], ACT.Abs)
+        nc.vector.scalar_tensor_tensor(hid[:, lo, :], woven[:, lo, :], -1.0, woven[:, lo, :], ALU.mult, ALU.max)
+        hid_codes = sbuf("hid_codes", [P, O], U32)
+        hid_plane = sbuf("hid_plane", [P, O], U8)
+        nc.vector.quantize_mx(hid_codes[:].bitcast(E5M2), hid_plane[:], hid[:].rearrange("p o t -> p (o t)"))
+
+        p_rows = [sbuf("p_rows%d" % h, [P, O], F32) for h in range(2)]
+        for h in range(2):
+            bank = psum.tile([P, O], F32, name="p_bank%d" % h)
+            nc.tensor.matmul_mx(
+                bank[:], lhsT=wb_all[:, 2 * P * h : 2 * P * (h + 1)].bitcast(E2M1),
+                lhsT_scale=wb_plane[:, P * h : P * (h + 1)],
+                rhs=hid_codes[:].bitcast(E5M2), rhs_scale=hid_plane[:], start=True, stop=True,
+            )
+            if h == 0:
+                nc.vector.tensor_copy(p_rows[h][:], bank[:])
+            else:
+                nc.scalar.copy(p_rows[h][:], bank[:])
+        for h in range(2):
+            nc.vector.tensor_copy(pages[h][0][:].indirect(l6[:]), p_rows[h][:])
+            nc.scalar.activation(pages[h][1][:].indirect(l7[:]), p_rows[h][:], ACT.Copy)
+
+        def add_pages(engine, h, c0, c1, total):
+            engine.tensor_tensor(total[:, c0:c1], pages[h][0][:, c0:c1], pages[h][1][:, c0:c1], ALU.add)
+
+        total0 = sbuf("total0", [P, E], F32)
+        total1 = sbuf("total1", [P, E], F32)
+        add_pages(nc.gpsimd, 0, 0, POOL_COLS, total0)
+        add_pages(nc.vector, 0, POOL_COLS, E, total0)
+        nc.sync.dma_start(out[0:P, :], total0[:])
+        add_pages(nc.vector, 1, 0, E // 2, total1)
+        nc.sync.dma_start(out[P:N, 0 : E // 2], total1[:, 0 : E // 2])
+        add_pages(nc.vector, 1, E // 2, E, total1)
+        nc.scalar.dma_start(out[P:N, E // 2 : E], total1[:, E // 2 : E])

@@ -70,6 +70,11 @@ def tile_list_gatedless_bank_one_pagetwice_kernel(
         xo_rows = xo_scales[0].bitcast(I32).rearrange("(u v i) c -> v i u c", u=2, v=2)
         for v in range(2):
             nc.scalar.dma_start(xo_stage[32 * v : 32 * v + 4, :, :], xo_rows[v])
+        warm_in = sbuf("warm_in", [P, 1], F32)
+        warm_out = sbuf("warm_out", [P, 1], F32)
+        nc.vector.memset(warm_in[:], 0.0)
+        nc.scalar.activation(warm_out[:], warm_in[:], ACT.Sigmoid)
+
         w0_all = sbuf("w0_all", [P, R], U16)
         nc.sync.dma_start(w0_all[:].bitcast(I32), w0_words[0].bitcast(I32))
         w_all = sbuf("w_all", [P, R], I32)

from contextlib import ExitStack

import concourse.mybir as mybir

K, T, J, R, F, Z, O, N, E = 512, 1024, 256, 512, 512, 1024, 128, 256, 512
FLOPS = 2 * K * R * J + 2 * F * R * J + 2 * R * N * O

F32 = mybir.dt.float32
BF16 = mybir.dt.bfloat16
I32 = mybir.dt.int32
U32 = mybir.dt.uint32
U16 = mybir.dt.uint16
U8 = mybir.dt.uint8
E4M3 = mybir.dt.float8_e4m3fn_x4
E5M2 = mybir.dt.float8_e5m2_x4
E2M1 = mybir.dt.float4_e2m1fn_x4
ACT = mybir.ActivationFunctionType
ALU = mybir.AluOpType

P = 128
PACK = 4
QUADS = 4
POOL_COLS = 384


def tile_list_gatedless_bank_one_pagetwice_kernel(
    tc, xt_words, xt_scales, xo_words, xo_scales, w_words, w_scales, w0_words, w0_scales,
    sa, sb, sg, bg, wb_words, wb_scales, offs, offs2, offs3, offs4, offs5, offs6, offs7, out,
):
    nc = tc.nc
    with ExitStack() as ctx:
        keep = ctx.enter_context(tc.tile_pool(name="keep", bufs=1))
        psum = ctx.enter_context(tc.psum_pool(name="psum", bufs=1))

        def sbuf(name, shape, dtype):
            return keep.tile(shape, dtype, name=name, align_bytes=64)

        def load_list(name, src):
            tile = keep.tile(list(src.shape), U16, name=name)
            nc.sync.dma_start(tile[:], src)
            return tile

        def load_rows(name, src, queue):
            tile = sbuf(name, [P, PACK], F32)
            queue.dma_start(tile[:], src.rearrange("(p t) one -> p (t one)", t=PACK))
            return tile

        def load_scale_rows(plane, src, quads, queue):
            rows = src[0].bitcast(I32)
            for q in quads:
                queue.dma_start(plane[:].bitcast(I32)[32 * q : 32 * q + 4, :], rows[4 * q : 4 * q + 4, :])

        xo_stage = sbuf("xo_stage", [P // 2, 2, Z // 4], I32)
        xt_plane = sbuf("xt_plane", [P, T], U8)
        w_raw = sbuf("w_raw", [P, 2 * R], U8)
        wb_plane = sbuf("wb_plane", [P, N], U8)
        nc.gpsimd.memset(xo_stage[:], 0)
        for plane in (xt_plane, w_raw, wb_plane):
            nc.vector.memset(plane[:].bitcast(I32), 0)

        l2 = load_list("l2", offs2)
        l1 = load_list("l1", offs)
        xo_all = sbuf("xo_all", [P, Z], I32)
        nc.sync.dma_start(xo_all[:], xo_words[0].rearrange("p c i -> p (c i)").bitcast(I32))
        xt_all = sbuf("xt_all", [P, T], U16)
        nc.sync.dma_start(xt_all[:].bitcast(I32), xt_words[0].bitcast(I32))
        stage = sbuf("stage", [4, QUADS, 2 * R // 4], I32)
        nc.scalar.dma_start(stage[:, :, 0 : R // 4], w0_scales[0].bitcast(I32).rearrange("(q i) c -> i q c", i=4))
        nc.scalar.dma_start(stage[:, :, R // 4 :], w_scales[0].bitcast(I32).rearrange("(q i) c -> i q c", i=4))
        xo_rows = xo_scales[0].bitcast(I32).rearrange("(u v i) c -> v i u c", u=2, v=2)
        for v in range(2):
            nc.scalar.dma_start(xo_stage[32 * v : 32 * v + 4, :, :], xo_rows[v])
        warm_in = sbuf("warm_in", [P, 1], F32)
        warm_out = sbuf("warm_out", [P, 1], F32)
        nc.vector.memset(warm_in[:], 0.0)
        nc.scalar.activation(warm_out[:], warm_in[:], ACT.Sigmoid)

        w0_all = sbuf("w0_all", [P, R], U16)
        nc.sync.dma_start(w0_all[:].bitcast(I32), w0_words[0].bitcast(I32))
        w_all = sbuf("w_all", [P, R], I32)
        nc.sync.dma_start(w_all[:], w_words[0].rearrange("p c i -> p (c i)").bitcast(I32))
        load_scale_rows(xt_plane, xt_scales, range(QUADS), nc.sync)
        l4 = load_list("l4", offs4)
        sg_t = load_rows("sg_t", sg, nc.sync)
        bg_t = load_rows("bg_t", bg, nc.sync)
        l3 = load_list("l3", offs3)
        sa_t = load_rows("sa_t", sa, nc.sync)
        l5 = load_list("l5", offs5)
        sb_t = load_rows("sb_t", sb, nc.sync)
        wb_all = sbuf("wb_all", [P, 2 * N], U8)
        nc.sync.dma_start(wb_all[:].bitcast(I32), wb_words[0].bitcast(I32))
        load_scale_rows(wb_plane, wb_scales, range(QUADS), nc.sync)
        l6 = load_list("l6", offs6)
        l7 = load_list("l7", offs7)

        pages = [[sbuf("page%d%d" % (h, s), [P, E], F32) for s in range(2)] for h in range(2)]
        for s in range(2):
            nc.vector.memset(pages[0][s][:], 0.0)
            nc.gpsimd.memset(pages[1][s][:], 0.0)

        for q in range(QUADS):
            nc.vector.tensor_copy(w_raw[:].bitcast(I32)[32 * q : 32 * q + 4, :], stage[:, q, :])
        w0_plane = sbuf("w0_plane", [P, R], U8)
        w_plane = sbuf("w_plane", [P, R], U8)
        for plane, c0 in ((w0_plane, 0), (w_plane, R)):
            nc.gpsimd.tensor_copy(
                plane[:].rearrange("p (t m) -> p t m", t=PACK),
                w_raw[:, c0 : c0 + R].rearrange("p (m t) -> p t m", t=PACK),
            )
        w0_codes = sbuf("w0_codes", [P, R], U16)
        nc.scalar.copy(
            w0_codes[:].rearrange("p (t m) -> p m t", t=PACK), w0_all[:].rearrange("p (m t) -> p m t", t=PACK)
        )
        w_codes = sbuf("w_codes", [P, R], U32)
        nc.scalar.copy(
            w_codes[:].rearrange("p (t m) -> p m t", t=PACK),
            w_all[:].bitcast(U32).rearrange("p (m t) -> p m t", t=PACK),
        )

        xo_plane = sbuf("xo_plane", [P, Z], U8)
        for u in range(2):
            nc.vector.tensor_copy(xo_plane[:].bitcast(I32)[64 * u : 64 * (u + 1), :], xo_stage[:, u, :])
        xo_picked = sbuf("xo_picked", [P, J], U8)
        nc.vector.tensor_copy(xo_picked[:], xo_plane[:].indirect(l2[:]))
        xo_codes = sbuf("xo_codes", [P, J], U32)
        nc.vector.tensor_copy(xo_codes[:], xo_all[:].bitcast(U32).indirect(l2[:]))
        xt_codes = sbuf("xt_codes", [P, J], U16)
        nc.vector.tensor_copy(xt_codes[:], xt_all[:].indirect(l1[:]))
        xt_picked = sbuf("xt_picked", [P, J], U8)
        nc.vector.tensor_copy(xt_picked[:], xt_plane[:].indirect(l1[:]))

        banks = [psum.tile([P, J], F32, name="a_bank%d" % t) for t in range(PACK)]
        for t in range(PACK):
            cols = slice(t * P, (t + 1) * P)
            nc.tensor.matmul_mx(
                banks[t][:], lhsT=w0_codes[:, cols].bitcast(E2M1), lhsT_scale=w0_plane[:, cols],
                rhs=xo_codes[:].bitcast(E4M3), rhs_scale=xo_picked[:], start=True, stop=False,
            )
            nc.tensor.matmul_mx(
                banks[t][:], lhsT=w_codes[:, cols].bitcast(E4M3), lhsT_scale=w_plane[:, cols],
                rhs=xt_codes[:].bitcast(E2M1), rhs_scale=xt_picked[:], start=False, stop=True,
            )

        gate = sbuf("gate", [P, PACK, O], F32)
        first = sbuf("first", [P, PACK, O], F32)
        second = sbuf("second", [P, PACK, O], F32)
        gated = sbuf("gated", [P, PACK, O], F32)
        diff = sbuf("diff", [P, PACK, O], F32)
        a_rows = [sbuf("a_rows%d" % t, [P, J], F32) for t in range(PACK)]
        for t in range(PACK):
            nc.vector.tensor_copy(a_rows[t][:], banks[t][:])
        for t in range(PACK):
            col = slice(t, t + 1)
            nc.scalar.activation(
                gate[:, t, :], a_rows[t][:].indirect(l4[:]), ACT.Sigmoid, bias=bg_t[:, col], scale=sg_t[:, col]
            )
            nc.scalar.activation(first[:, t, :], a_rows[t][:].indirect(l3[:]), ACT.Copy, scale=sa_t[:, col])
            nc.vector.tensor_tensor(gated[:, t, :], first[:, t, :], gate[:, t, :], ALU.mult)
            nc.scalar.activation(second[:, t, :], a_rows[t][:].indirect(l5[:]), ACT.Copy, scale=sb_t[:, col])
            nc.vector.tensor_tensor(diff[:, t, :], gated[:, t, :], second[:, t, :], ALU.subtract)

        hid = sbuf("hid", [P, O, PACK], BF16)
        woven = diff[:].rearrange("p t o -> p o t")
        lo, hi = slice(0, O // 2), slice(O // 2, O)
        nc.scalar.activation(hid[:, hi, :], woven[:, hi, :], ACT.Abs)
        nc.vector.scalar_tensor_tensor(hid[:, lo, :], woven[:, lo, :], -1.0, woven[:, lo, :], ALU.mult, ALU.max)
        hid_codes = sbuf("hid_codes", [P, O], U32)
        hid_plane = sbuf("hid_plane", [P, O], U8)
        nc.vector.quantize_mx(hid_codes[:].bitcast(E5M2), hid_plane[:], hid[:].rearrange("p o t -> p (o t)"))

        p_rows = [sbuf("p_rows%d" % h, [P, O], F32) for h in range(2)]
        for h in range(2):
            bank = psum.tile([P, O], F32, name="p_bank%d" % h)
            nc.tensor.matmul_mx(
                bank[:], lhsT=wb_all[:, 2 * P * h : 2 * P * (h + 1)].bitcast(E2M1),
                lhsT_scale=wb_plane[:, P * h : P * (h + 1)],
                rhs=hid_codes[:].bitcast(E5M2), rhs_scale=hid_plane[:], start=True, stop=True,
            )
            if h == 0:
                nc.vector.tensor_copy(p_rows[h][:], bank[:])
            else:
                nc.scalar.copy(p_rows[h][:], bank[:])
        for h in range(2):
            nc.vector.tensor_copy(pages[h][0][:].indirect(l6[:]), p_rows[h][:])
            nc.scalar.activation(pages[h][1][:].indirect(l7[:]), p_rows[h][:], ACT.Copy)

        def add_pages(engine, h, c0, c1, total):
            engine.tensor_tensor(total[:, c0:c1], pages[h][0][:, c0:c1], pages[h][1][:, c0:c1], ALU.add)

        total0 = sbuf("total0", [P, E], F32)
        total1 = sbuf("total1", [P, E], F32)
        add_pages(nc.gpsimd, 0, 0, POOL_COLS, total0)
        add_pages(nc.vector, 0, POOL_COLS, E, total0)
        nc.sync.dma_start(out[0:P, :], total0[:])
        add_pages(nc.vector, 1, 0, E // 2, total1)
        nc.sync.dma_start(out[P:N, 0 : E // 2], total1[:, 0 : E // 2])
        add_pages(nc.vector, 1, E // 2, E, total1)
        nc.scalar.dma_start(out[P:N, E // 2 : E], total1[:, E // 2 : E])
